import numpy as np
import ml_dtypes


def mxq(x, axis, fmt="e4m3"):
    dtype, down = {"e4m3": (ml_dtypes.float8_e4m3fn, 7), "e5m2": (ml_dtypes.float8_e5m2, 14)}[fmt]
    v = np.moveaxis(np.asarray(x, np.float32).astype(ml_dtypes.bfloat16).astype(np.float64), axis, -1)
    blocks = v.reshape(v.shape[:-1] + (-1, 32))
    amax = np.abs(blocks).max(-1, keepdims=True)
    byte = np.maximum(np.where(amax > 0, np.frexp(amax)[1] - 1 + 127, 0) - down, 1)
    scale = np.exp2(byte - 127.0)
    codes = (blocks / scale).astype(np.float32).astype(dtype).astype(np.float64)
    return np.moveaxis((codes * scale).reshape(v.shape), -1, axis)


WIDE = False


def mx_kscale(k):
    if not WIDE:
        return np.ones(k)
    levels = np.array([10, -10, 5, -5, 0])
    if k % 512:
        return np.exp2(np.random.permutation(np.resize(levels, k // 32))).repeat(32)
    a = np.empty((k // 512, 16))
    for p in range(k // 512):
        a[p, :8] = np.random.permutation(np.resize(levels, 8))
        for g in range(8):
            far = levels[np.abs(levels - a[p, g]) >= 10]
            a[p, g + 8] = far[np.random.randint(len(far))]
    return np.exp2(a.ravel()).repeat(32)


def f64(x):
    return np.asarray(x).astype(np.float64)


def striped(idx):
    return np.tile(idx.reshape(-1, 16).T, (8, 1)).astype(np.uint16)


def unstriped(offs):
    return offs[:16].T.reshape(-1).astype(np.int64)


def striped8(idx):
    return np.concatenate([x.reshape(-1, 16).T for x in idx]).astype(np.uint16)


def runs(offs, k):
    lists = np.stack([offs[16 * r : 16 * r + 16].T.reshape(-1) for r in range(8)]).astype(np.int64)
    return lists[np.arange(k) % 512 // 64]


def pack_weight(w):
    k, n = w.shape
    w = f64(np.asarray(w, np.float32).astype(ml_dtypes.bfloat16)).reshape(k // 32, 32, n)
    amax = np.abs(w).max(1)
    byte = np.clip(np.where(amax > 0, np.frexp(amax)[1] - 1 + 127 - 7, 1), 1, 254)
    scaled = (w * np.exp2(127.0 - byte)[:, None, :]).reshape(k, n).astype(np.float32)
    words = np.ascontiguousarray(scaled.reshape(k // 512, 128, 4, n).transpose(0, 1, 3, 2)).astype(ml_dtypes.float8_e4m3fn).view(np.uint8)
    return words, np.ascontiguousarray(byte.astype(np.uint8).reshape(k // 512, 16, n))


def unpack_weight(words, scales):
    g, p, n, _ = words.shape
    vals = np.ascontiguousarray(words).view(ml_dtypes.float8_e4m3fn).astype(np.float64) * np.repeat(np.exp2(scales.astype(np.float64) - 127.0), 8, axis=1)[..., None]
    return vals.transpose(0, 1, 3, 2).reshape(g * 512, n)


def sigmoid(v):
    return 1.0 / (1.0 + np.exp(-np.maximum(v, -700.0)))

def planes(y):
    n, m = y.shape
    v = y.astype(np.float32).astype(ml_dtypes.bfloat16).astype(np.float64).reshape(n // 32, 32, m)
    top = np.abs(v).max(1)
    byte = np.clip(np.where(top > 0, np.frexp(top)[1] - 1 + 127 - 7, 1), 1, 254)
    codes = (v * np.exp2(127.0 - byte)[:, None, :]).reshape(n, m).astype(np.float32).astype(ml_dtypes.float8_e4m3fn).view(np.uint8)
    words = codes.reshape(n // 512, 128, 4, m).transpose(0, 1, 3, 2)
    return np.ascontiguousarray(words), np.ascontiguousarray(byte.astype(np.uint8).reshape(n // 512, 16, m))


K, T, S, N, H, W = 512, 2048, 512, 512, 512, 256


def setup_inputs():
    n = np.random.standard_normal
    s = mx_kscale(K)[:, None]
    u = mx_kscale(S)
    packed_xT = pack_weight(n((K, T)) * s)
    perm = np.stack([np.random.permutation(H) for _ in range(8)])
    return {
        "x_words": packed_xT[0],
        "x_scales": packed_xT[1],
        "wa": (n((K, H)) / np.sqrt(K) / s).astype(np.float32),
        "wb": (n((K, N)) / np.sqrt(K) / s).astype(np.float32),
        "gt": (np.random.uniform(0.5, 1.5, (S, 1)) * u[:, None]).astype(np.float32),
        "gi": (np.random.uniform(0.5, 1.5, (S, 1)) / u[:, None]).astype(np.float32),
        "offs": striped(np.random.permutation(T)[:S]),
        "two": striped(np.random.permutation(T)[:S]),
        "n1": striped8(perm[:, :W]),
        "n2": striped8(perm[:, W:]),
        "n3": striped8(np.stack([np.random.permutation(N) for _ in range(8)])),
        "n4": striped8(np.stack([np.random.permutation(N) for _ in range(8)])),
    }


def reference(x_words, x_scales, wa, wb, gt, gi, offs, two, n1, n2, n3, n4):
    xq = unpack_weight(x_words, x_scales)[:, unstriped(offs)]
    a = xq.T @ mxq(f64(wa), 0, "e4m3")
    pa = a[np.arange(S)[:, None], runs(n1, S)]
    pb = a[np.arange(S)[:, None], runs(n2, S)]
    rb = pa * pb
    ra = pa + pb
    ds = np.zeros((S, H))
    ds[np.arange(S)[:, None], runs(n1, S)] = ra
    dt = ds.copy()
    dt[np.arange(S)[:, None], runs(n2, S)] = rb
    z = f64(gt) * dt
    x_two = unpack_weight(x_words, x_scales)[:, unstriped(two)]
    b = x_two.T @ mxq(f64(wb), 0, "e4m3")
    z2 = f64(gi) * b
    cv = 0.0625 * ((mxq(z, 0, "e4m3").T @ mxq(z2, 0, "e4m3")))
    out_0 = (cv - (cv[np.arange(H)[:, None], runs(n3, H)])) * (sigmoid(cv[np.arange(H)[:, None], runs(n4, H)]))
    return (out_0,) + planes(out_0)

@@ -1,0 +1,243 @@
+from contextlib import ExitStack
+
+import concourse.mybir as mybir
+from concourse.masks import make_identity
+
+K, T, S, N, H, W = 512, 2048, 512, 512, 512, 256
+FLOPS = 2 * (K * S * H + K * S * N + S * H * N)
+
+F32 = mybir.dt.float32
+BF16 = mybir.dt.bfloat16
+I32 = mybir.dt.int32
+U32 = mybir.dt.uint32
+U16 = mybir.dt.uint16
+U8 = mybir.dt.uint8
+FP8X4 = mybir.dt.float8_e4m3fn_x4
+ALU = mybir.AluOpType
+ACT = mybir.ActivationFunctionType
+
+P = 128
+PACK = 4
+HALF = 256
+
+
+def tile_picked_mombondgdif_none_po_kernel(
+    tc, x_words, x_scales, wa, wb, gt, gi, offs, two, n1, n2, n3, n4, out_0, out_1, out_2
+):
+    nc = tc.nc
+    with ExitStack() as ctx:
+        sb = ctx.enter_context(tc.tile_pool(name="sb", bufs=1))
+        ps = ctx.enter_context(tc.psum_pool(name="ps", bufs=1))
+
+        def tile(shape, dtype, name, tag=""):
+            return sb.tile(shape, dtype, name=name, tag=tag, align_bytes=64)
+
+        def load_list(src, name):
+            t = tile([P, src.shape[1]], U16, name)
+            nc.sync.dma_start(t[:], src)
+            return t
+
+        def interleave(copy, grouped, planes):
+            copy(
+                out=grouped.rearrange("p (c i) t -> p c t i", i=4),
+                in_=planes.rearrange("p t (c i) -> p c t i", i=4),
+            )
+
+        def quantize(codes, scales, grouped):
+            nc.vector.quantize_mx(out=codes.bitcast(FP8X4), scales=scales, in_=grouped)
+
+        def product(bank, lhs_codes, lhs_scales, t, rhs_codes, rhs_scales):
+            cols = slice(P * t, P * (t + 1))
+            nc.tensor.matmul_mx(
+                out=bank[:],
+                lhsT=lhs_codes[:, cols].bitcast(FP8X4),
+                lhsT_scale=lhs_scales[:, cols],
+                rhs=rhs_codes[:].bitcast(FP8X4),
+                rhs_scale=rhs_scales[:],
+                start=True,
+                stop=True,
+            )
+
+        xs = tile([P, T], U8, "xs")
+        nc.gpsimd.memset(xs[:].bitcast(I32), 0)
+        offs_t = load_list(offs, "offs_t")
+        two_t = load_list(two, "two_t")
+        wa_rows = wa.rearrange("(p j) c -> p j c", j=PACK)
+        wa_raw = [tile([P, PACK, HALF], F32, f"wa_raw{h}") for h in range(2)]
+        nc.sync.dma_start(wa_raw[0][:], wa_rows[:, :, :HALF])
+        xs_rows = x_scales[0].bitcast(I32)
+        for q in range(4):
+            nc.sync.dma_start(xs[32 * q : 32 * q + 4, :].bitcast(I32), xs_rows[4 * q : 4 * q + 4, :])
+        xw = tile([P, T], U32, "xw")
+        nc.sync.dma_start(xw[:].bitcast(I32), x_words[0].rearrange("p c r -> p (c r)").bitcast(I32))
+        nc.sync.dma_start(wa_raw[1][:], wa_rows[:, :, HALF:])
+        wb_rows = wb.rearrange("(p j) c -> p j c", j=PACK)
+        wb_raw = [tile([P, PACK, HALF], F32, f"wb_raw{h}") for h in range(2)]
+        for h in range(2):
+            nc.sync.dma_start(wb_raw[h][:], wb_rows[:, :, HALF * h : HALF * (h + 1)])
+        n1_t = load_list(n1, "n1_t")
+        n2_t = load_list(n2, "n2_t")
+        identity = tile([P, P], F32, "identity")
+        make_identity(nc, identity[:])
+        weight_rows = []
+        for name, src in (("gi_rows", gi), ("gt_rows", gt)):
+            rows = tile([P, P], F32, name)
+            nc.gpsimd.memset(rows[:], 0.0)
+            nc.sync.dma_start(
+                rows[:PACK, :].rearrange("t (q r) -> t q r", r=8),
+                src.rearrange("(q t r) o -> t q (r o)", t=PACK, r=8),
+            )
+            weight_rows.append(rows)
+
+        def turn_weights(rows, name, tag):
+            turned = ps.tile([P, P], F32, name=name + "_turned", tag=tag)
+            nc.tensor.transpose(turned[:], rows[:], identity[:])
+            weights = tile([P, PACK], F32, name)
+            nc.scalar.copy(weights[:], turned[:, :PACK])
+            return weights
+
+        n3_t = load_list(n3, "n3_t")
+        n4_t = load_list(n4, "n4_t")
+
+        def pick_scales(lst, name):
+            picked = tile([P, S], U8, name + "_picked")
+            nc.vector.tensor_copy(picked[:], xs[:].indirect(lst[:]))
+            dealt = tile([P, S], U8, name + "_dealt")
+            nc.vector.tensor_copy(
+                dealt[:].bitcast(I32).rearrange("p (t q w) -> p q t w", t=PACK, w=2),
+                picked[:].bitcast(I32).rearrange("p (q t w) -> p q t w", t=PACK, w=2),
+            )
+            return dealt
+
+        def pick_words(lst, name):
+            picked = tile([P, S], U32, name)
+            nc.vector.tensor_copy(picked[:].rearrange("p (t q r) -> p q t r", t=PACK, r=8), xw[:].indirect(lst[:]))
+            return picked
+
+        xa_s = pick_scales(offs_t, "xa_s")
+        xb_s = pick_scales(two_t, "xb_s")
+        xa_w = pick_words(offs_t, "xa_w")
+
+        wa_g = [tile([P, HALF, PACK], BF16, f"wa_g{h}") for h in range(2)]
+        wa_q = tile([P, H], U32, "wa_q")
+        wa_s = tile([P, H], U8, "wa_s")
+        interleave(nc.scalar.copy, wa_g[0][:], wa_raw[0][:])
+        interleave(nc.vector.tensor_copy, wa_g[1][:], wa_raw[1][:])
+        for h in range(2):
+            cols = slice(HALF * h, HALF * (h + 1))
+            quantize(wa_q[:, cols], wa_s[:, cols], wa_g[h][:].rearrange("p c t -> p (c t)"))
+        a_banks = [ps.tile([P, H], F32, name=f"a{t}", tag=f"first{t}") for t in range(PACK)]
+        for t in range(PACK):
+            product(a_banks[t], xa_w, xa_s, t, wa_q, wa_s)
+
+        xb_w = pick_words(two_t, "xb_w")
+        wb_g = [tile([P, HALF, PACK], BF16, f"wb_g{h}") for h in range(2)]
+        wb_q = tile([P, N], U32, "wb_q")
+        wb_s = tile([P, N], U8, "wb_s")
+        for h in range(2):
+            interleave(nc.vector.tensor_copy, wb_g[h][:], wb_raw[h][:])
+        gi_t = turn_weights(weight_rows[0], "gi_t", "second3")
+
+        pa, pb, dt = [], [], []
+        for t in range(PACK):
+            a_t = tile([P, H], F32, f"a_sb{t}")
+            nc.scalar.copy(a_t[:], a_banks[t][:])
+            pa.append(tile([P, W], F32, f"pa{t}"))
+            pb.append(tile([P, W], F32, f"pb{t}"))
+            nc.scalar.activation(pa[t][:], a_t[:].indirect(n1_t[:]), ACT.Copy)
+            nc.scalar.activation(pb[t][:], a_t[:].indirect(n2_t[:]), ACT.Copy)
+
+        def put_sum(t):
+            dt.append(tile([P, H], F32, f"dt{t}", tag="late" if t == PACK - 1 else ""))
+            nc.vector.tensor_tensor(dt[t][:].indirect(n1_t[:]), pa[t][:], pb[t][:], ALU.add)
+
+        def put_product(t):
+            nc.vector.tensor_tensor(dt[t][:].indirect(n2_t[:]), pa[t][:], pb[t][:], ALU.mult)
+
+        put_sum(0)
+        for h in range(2):
+            cols = slice(HALF * h, HALF * (h + 1))
+            quantize(wb_q[:, cols], wb_s[:, cols], wb_g[h][:].rearrange("p c t -> p (c t)"))
+        b_banks = [ps.tile([P, N], F32, name=f"b{t}", tag=f"second{t}") for t in range(PACK)]
+        for t in range(PACK):
+            product(b_banks[t], xb_w, xb_s, t, wb_q, wb_s)
+        z2_pairs = tile([P, 2, N, 2], BF16, "z2_pairs")
+        for t in range(PACK):
+            nc.scalar.activation(z2_pairs[:, t // 2, :, t % 2], b_banks[t][:], ACT.Copy, scale=gi_t[:, t : t + 1])
+        gt_t = turn_weights(weight_rows[1], "gt_t", "second3")
+
+        def merge_pairs(copy, word, grouped, pairs):
+            copy(
+                grouped[:].bitcast(word).rearrange("p (c i u) -> p c u i", i=2, u=2),
+                pairs[:].rearrange("p u c e -> p u (c e)").bitcast(word).rearrange("p u (c i) -> p c u i", i=2),
+            )
+
+        z_pairs = [tile([P, 2, HALF, 2], BF16, f"z_pairs{h}") for h in range(2)]
+
+        def weigh_z(t):
+            for h in range(2):
+                nc.scalar.activation(
+                    z_pairs[h][:, t // 2, :, t % 2].rearrange("p (a m) -> p m a", a=2),
+                    dt[t][:].rearrange("p (m a) -> p m a", a=PACK)[:, :, 2 * h : 2 * h + 2],
+                    ACT.Copy,
+                    scale=gt_t[:, t : t + 1],
+                )
+
+        z2_g = tile([P, N * PACK], BF16, "z2_g", tag="late")
+        z2_q = tile([P, N], U32, "z2_q")
+        z2_s = tile([P, N], U8, "z2_s")
+        merge_pairs(nc.scalar.copy, U32, z2_g, z2_pairs)
+        put_sum(1)
+        put_product(0)
+        weigh_z(0)
+        put_sum(2)
+        put_product(1)
+        weigh_z(1)
+        put_product(2)
+        weigh_z(2)
+        quantize(z2_q[:], z2_s[:], z2_g[:])
+        put_sum(3)
+        put_product(3)
+        weigh_z(3)
+
+        z_q = tile([P, H], U32, "z_q")
+        z_s = tile([P, H], U8, "z_s")
+        z_g = [tile([P, HALF * PACK], BF16, f"z_g{h}") for h in range(2)]
+        for h in range(2):
+            merge_pairs(nc.vector.tensor_copy, I32, z_g[h], z_pairs[h])
+        cv = []
+        for h in range(2):
+            cols = slice(HALF * h, HALF * (h + 1))
+            quantize(z_q[:, cols], z_s[:, cols], z_g[h][:])
+        for t in range(PACK):
+            bank = ps.tile([P, N], F32, name=f"cv{t}", tag=f"first{t}")
+            product(bank, z_q, z_s, t, z2_q, z2_s)
+            cv.append(tile([P, N], F32, f"cv_sb{t}"))
+            nc.vector.tensor_scalar(cv[t][:], bank[:], 0.0625, None, ALU.mult)
+
+        y_rows = out_0.rearrange("(p t) c -> p t c", t=PACK)
+        y_words = out_1[0].rearrange("p c r -> p (c r)").bitcast(I32)
+        y_scales = out_2[0].bitcast(I32)
+        y_q = tile([P, N], U32, "y_q")
+        y_s = tile([P, N], U8, "y_s")
+        for first, width in ((0, 256), (256, 128), (384, 128)):
+            cols = slice(first, first + width)
+            entries = slice(first // 16, (first + width) // 16)
+            y = tile([P, PACK, width], F32, f"y{first}")
+            for t in range(PACK):
+                other = tile([P, width], F32, f"other{first}_{t}")
+                gate = tile([P, width], F32, f"gate{first}_{t}")
+                diff = tile([P, width], F32, f"diff{first}_{t}")
+                fetches = [(other, n3_t, ACT.Copy), (gate, n4_t, ACT.Sigmoid)]
+                for fetched, lst, func in fetches[::-1] if first == 0 else fetches:
+                    nc.scalar.activation(fetched[:], cv[t][:].indirect(lst[:, entries]), func)
+                nc.vector.tensor_tensor(diff[:], cv[t][:, cols], other[:], ALU.subtract)
+                nc.vector.tensor_tensor(y[:, t, :], diff[:], gate[:], ALU.mult)
+            nc.sync.dma_start(y_rows[:, :, cols], y[:])
+            y_g = tile([P, width, PACK], BF16, f"y_g{first}")
+            interleave(nc.vector.tensor_copy, y_g[:], y[:])
+            quantize(y_q[:, cols], y_s[:, cols], y_g[:].rearrange("p c t -> p (c t)"))
+            nc.sync.dma_start(y_words[:, cols], y_q[:, cols].bitcast(I32))
+        for q in range(4):
+            queue = nc.scalar if q % 2 else nc.sync
+            queue.dma_start(y_scales[4 * q : 4 * q + 4, :], y_s[32 * q : 32 * q + 4, :].bitcast(I32))

@@ -49,11 +49,11 @@ def tile_picked_mombondgdif_none_po_kernel(
         def product(bank, lhs_codes, lhs_scales, t, rhs_codes, rhs_scales):
             cols = slice(P * t, P * (t + 1))
             nc.tensor.matmul_mx(
-                out=bank[:],
+                out=bank,
                 lhsT=lhs_codes[:, cols].bitcast(FP8X4),
                 lhsT_scale=lhs_scales[:, cols],
-                rhs=rhs_codes[:].bitcast(FP8X4),
-                rhs_scale=rhs_scales[:],
+                rhs=rhs_codes.bitcast(FP8X4),
+                rhs_scale=rhs_scales,
                 start=True,
                 stop=True,
             )
@@ -63,20 +63,22 @@ def tile_picked_mombondgdif_none_po_kernel(
         offs_t = load_list(offs, "offs_t")
         two_t = load_list(two, "two_t")
         wa_rows = wa.rearrange("(p j) c -> p j c", j=PACK)
-        wa_raw = [tile([P, PACK, HALF], F32, f"wa_raw{h}") for h in range(2)]
-        nc.sync.dma_start(wa_raw[0][:], wa_rows[:, :, :HALF])
+        wa_cols = [slice(0, 256), slice(256, 384), slice(384, 512)]
+        wa_raw = [tile([P, PACK, c.stop - c.start], F32, f"wa_raw{c.start}", tag="a_rows" if c.stop == H else "") for c in wa_cols]
+        nc.sync.dma_start(wa_raw[0][:], wa_rows[:, :, wa_cols[0]])
         xs_rows = x_scales[0].bitcast(I32)
         for q in range(4):
             nc.sync.dma_start(xs[32 * q : 32 * q + 4, :].bitcast(I32), xs_rows[4 * q : 4 * q + 4, :])
         xw = tile([P, T], U32, "xw")
         nc.sync.dma_start(xw[:].bitcast(I32), x_words[0].rearrange("p c r -> p (c r)").bitcast(I32))
-        nc.sync.dma_start(wa_raw[1][:], wa_rows[:, :, HALF:])
-        wb_rows = wb.rearrange("(p j) c -> p j c", j=PACK)
-        wb_raw = [tile([P, PACK, HALF], F32, f"wb_raw{h}") for h in range(2)]
-        for h in range(2):
-            nc.sync.dma_start(wb_raw[h][:], wb_rows[:, :, HALF * h : HALF * (h + 1)])
+        for i in (1, 2):
+            nc.sync.dma_start(wa_raw[i][:], wa_rows[:, :, wa_cols[i]])
         n1_t = load_list(n1, "n1_t")
         n2_t = load_list(n2, "n2_t")
+        wb_rows = wb.rearrange("(p j) c -> p j c", j=PACK)
+        wb_raw = [tile([P, PACK, HALF], F32, f"wb_raw{h}", tag="" if h else "wb_first") for h in range(2)]
+        for h in range(2):
+            nc.sync.dma_start(wb_raw[h][:], wb_rows[:, :, HALF * h : HALF * (h + 1)])
         identity = tile([P, P], F32, "identity")
         make_identity(nc, identity[:])
         weight_rows = []
@@ -99,56 +101,65 @@ def tile_picked_mombondgdif_none_po_kernel(
         n3_t = load_list(n3, "n3_t")
         n4_t = load_list(n4, "n4_t")
 
-        def pick_scales(lst, name):
+        def pick_scales(lst, name, tag=""):
             picked = tile([P, S], U8, name + "_picked")
             nc.vector.tensor_copy(picked[:], xs[:].indirect(lst[:]))
-            dealt = tile([P, S], U8, name + "_dealt")
+            dealt = tile([P, S], U8, name + "_dealt", tag=tag)
             nc.vector.tensor_copy(
                 dealt[:].bitcast(I32).rearrange("p (t q w) -> p q t w", t=PACK, w=2),
                 picked[:].bitcast(I32).rearrange("p (q t w) -> p q t w", t=PACK, w=2),
             )
             return dealt
 
-        def pick_words(lst, name):
-            picked = tile([P, S], U32, name)
+        def pick_words(lst, name, tag=""):
+            picked = tile([P, S], U32, name, tag=tag)
             nc.vector.tensor_copy(picked[:].rearrange("p (t q r) -> p q t r", t=PACK, r=8), xw[:].indirect(lst[:]))
             return picked
 
-        xa_s = pick_scales(offs_t, "xa_s")
+        xa_s = pick_scales(offs_t, "xa_s", tag="xa_s")
         xb_s = pick_scales(two_t, "xb_s")
         xa_w = pick_words(offs_t, "xa_w")
 
-        wa_g = [tile([P, HALF, PACK], BF16, f"wa_g{h}") for h in range(2)]
         wa_q = tile([P, H], U32, "wa_q")
         wa_s = tile([P, H], U8, "wa_s")
-        interleave(nc.scalar.copy, wa_g[0][:], wa_raw[0][:])
-        interleave(nc.vector.tensor_copy, wa_g[1][:], wa_raw[1][:])
-        for h in range(2):
-            cols = slice(HALF * h, HALF * (h + 1))
-            quantize(wa_q[:, cols], wa_s[:, cols], wa_g[h][:].rearrange("p c t -> p (c t)"))
         a_banks = [ps.tile([P, H], F32, name=f"a{t}", tag=f"first{t}") for t in range(PACK)]
-        for t in range(PACK):
-            product(a_banks[t], xa_w, xa_s, t, wa_q, wa_s)
+        a_early = ps.tile([P, HALF], F32, name="a_early", tag="second0")
+        for i, cols in enumerate(wa_cols):
+            wa_g = tile([P, cols.stop - cols.start, PACK], BF16, f"wa_g{i}", tag="wa_last" if i == 2 else "")
+            interleave(nc.scalar.copy, wa_g[:], wa_raw[i][:])
+            quantize(wa_q[:, cols], wa_s[:, cols], wa_g[:].rearrange("p c t -> p (c t)"))
+            product(a_early[:] if i == 0 else a_banks[0][:, cols], xa_w, xa_s, 0, wa_q[:, cols], wa_s[:, cols])
+        a_sb = [tile([P, H], F32, "a_sb0", tag="a_rows")]
+        nc.scalar.copy(a_sb[0][:, :HALF], a_early[:])
+        for t in range(1, PACK):
+            product(a_banks[t][:], xa_w, xa_s, t, wa_q[:], wa_s[:])
 
-        xb_w = pick_words(two_t, "xb_w")
-        wb_g = [tile([P, HALF, PACK], BF16, f"wb_g{h}") for h in range(2)]
+        xb_w = pick_words(two_t, "xb_w", tag="wa_last")
+        wb_g = [tile([P, HALF, PACK], BF16, f"wb_g{h}", tag="" if h else "xa_s") for h in range(2)]
         wb_q = tile([P, N], U32, "wb_q")
         wb_s = tile([P, N], U8, "wb_s")
-        for h in range(2):
-            interleave(nc.vector.tensor_copy, wb_g[h][:], wb_raw[h][:])
-        gi_t = turn_weights(weight_rows[0], "gi_t", "second3")
+        interleave(nc.scalar.copy, wb_g[0][:], wb_raw[0][:])
+        interleave(nc.vector.tensor_copy, wb_g[1][:], wb_raw[1][:])
 
         pa, pb, dt = [], [], []
         for t in range(PACK):
-            a_t = tile([P, H], F32, f"a_sb{t}")
-            nc.scalar.copy(a_t[:], a_banks[t][:])
+            if t > 0:
+                a_sb.append(tile([P, H], F32, f"a_sb{t}", tag="wb_first" if t == 2 else "a_rows"))
+            a_t = a_sb[t]
+            rest = slice(HALF if t == 0 else 0, H)
+            nc.scalar.copy(a_t[:, rest], a_banks[t][:, rest])
             pa.append(tile([P, W], F32, f"pa{t}"))
             pb.append(tile([P, W], F32, f"pb{t}"))
             nc.scalar.activation(pa[t][:], a_t[:].indirect(n1_t[:]), ACT.Copy)
-            nc.scalar.activation(pb[t][:], a_t[:].indirect(n2_t[:]), ACT.Copy)
+            if t == 0:
+                nc.vector.tensor_copy(pb[t][:], a_t[:].indirect(n2_t[:]))
+            else:
+                nc.scalar.activation(pb[t][:], a_t[:].indirect(n2_t[:]), ACT.Copy)
+
+        gi_t = turn_weights(weight_rows[0], "gi_t", "first3")
 
         def put_sum(t):
-            dt.append(tile([P, H], F32, f"dt{t}", tag="late" if t == PACK - 1 else ""))
+            dt.append(tile([P, H], F32, f"dt{t}"))
             nc.vector.tensor_tensor(dt[t][:].indirect(n1_t[:]), pa[t][:], pb[t][:], ALU.add)
 
         def put_product(t):
@@ -160,7 +171,7 @@ def tile_picked_mombondgdif_none_po_kernel(
             quantize(wb_q[:, cols], wb_s[:, cols], wb_g[h][:].rearrange("p c t -> p (c t)"))
         b_banks = [ps.tile([P, N], F32, name=f"b{t}", tag=f"second{t}") for t in range(PACK)]
         for t in range(PACK):
-            product(b_banks[t], xb_w, xb_s, t, wb_q, wb_s)
+            product(b_banks[t][:], xb_w, xb_s, t, wb_q[:], wb_s[:])
         z2_pairs = tile([P, 2, N, 2], BF16, "z2_pairs")
         for t in range(PACK):
             nc.scalar.activation(z2_pairs[:, t // 2, :, t % 2], b_banks[t][:], ACT.Copy, scale=gi_t[:, t : t + 1])
@@ -168,8 +179,8 @@ def tile_picked_mombondgdif_none_po_kernel(
 
         def merge_pairs(copy, word, grouped, pairs):
             copy(
-                grouped[:].bitcast(word).rearrange("p (c i u) -> p c u i", i=2, u=2),
-                pairs[:].rearrange("p u c e -> p u (c e)").bitcast(word).rearrange("p u (c i) -> p c u i", i=2),
+                grouped.bitcast(word).rearrange("p (c i u) -> p c u i", i=2, u=2),
+                pairs.rearrange("p u c e -> p u (c e)").bitcast(word).rearrange("p u (c i) -> p c u i", i=2),
             )
 
         z_pairs = [tile([P, 2, HALF, 2], BF16, f"z_pairs{h}") for h in range(2)]
@@ -183,37 +194,59 @@ def tile_picked_mombondgdif_none_po_kernel(
                     scale=gt_t[:, t : t + 1],
                 )
 
-        z2_g = tile([P, N * PACK], BF16, "z2_g", tag="late")
+        z2_g = tile([P, N * PACK], BF16, "z2_g")
         z2_q = tile([P, N], U32, "z2_q")
         z2_s = tile([P, N], U8, "z2_s")
-        merge_pairs(nc.scalar.copy, U32, z2_g, z2_pairs)
+        merge_pairs(nc.scalar.copy, U32, z2_g[:], z2_pairs[:])
         put_sum(1)
         put_product(0)
         weigh_z(0)
         put_sum(2)
         put_product(1)
         weigh_z(1)
+        put_sum(3)
         put_product(2)
         weigh_z(2)
-        quantize(z2_q[:], z2_s[:], z2_g[:])
-        put_sum(3)
         put_product(3)
+        quantize(z2_q[:], z2_s[:], z2_g[:])
         weigh_z(3)
 
         z_q = tile([P, H], U32, "z_q")
         z_s = tile([P, H], U8, "z_s")
-        z_g = [tile([P, HALF * PACK], BF16, f"z_g{h}") for h in range(2)]
-        for h in range(2):
-            merge_pairs(nc.vector.tensor_copy, I32, z_g[h], z_pairs[h])
-        cv = []
-        for h in range(2):
-            cols = slice(HALF * h, HALF * (h + 1))
-            quantize(z_q[:, cols], z_s[:, cols], z_g[h][:])
+        cv, gate = [], {}
+        cv_banks = [ps.tile([P, N], F32, name=f"cv{t}", tag=f"first{t}") for t in range(PACK)]
+        z_g = [tile([P, P * PACK], BF16, f"z_g{t}") for t in range(PACK)]
+
+        cv_early = ps.tile([P, HALF], F32, name="cv_early", tag="second0")
+
+        def finish_z(t):
+            cols = slice(P * t, P * (t + 1))
+            quantize(z_q[:, cols], z_s[:, cols], z_g[t][:])
+            if t == 0:
+                product(cv_early[:], z_q, z_s, t, z2_q[:, :HALF], z2_s[:, :HALF])
+                product(cv_banks[t][:, HALF:], z_q, z_s, t, z2_q[:, HALF:], z2_s[:, HALF:])
+            else:
+                product(cv_banks[t][:], z_q, z_s, t, z2_q[:], z2_s[:])
+
         for t in range(PACK):
-            bank = ps.tile([P, N], F32, name=f"cv{t}", tag=f"first{t}")
-            product(bank, z_q, z_s, t, z2_q, z2_s)
+            merge_pairs(nc.vector.tensor_copy, I32, z_g[t][:], z_pairs[t // 2][:, :, P * (t % 2) : P * (t % 2 + 1), :])
+            if t > 0:
+                finish_z(t - 1)
+        finish_z(PACK - 1)
+
+        def empty_bank(t):
             cv.append(tile([P, N], F32, f"cv_sb{t}"))
-            nc.vector.tensor_scalar(cv[t][:], bank[:], 0.0625, None, ALU.mult)
+            if t == 0:
+                nc.vector.tensor_scalar(cv[t][:, :HALF], cv_early[:], 0.0625, None, ALU.mult)
+                nc.vector.tensor_scalar(cv[t][:, HALF:], cv_banks[t][:, HALF:], 0.0625, None, ALU.mult)
+            elif t < PACK - 1:
+                nc.vector.tensor_scalar(cv[t][:], cv_banks[t][:], 0.0625, None, ALU.mult)
+            else:
+                nc.scalar.activation(cv[t][:], cv_banks[t][:], ACT.Copy, scale=0.0625)
+
+        def make_gate(t):
+            gate[t] = tile([P, N], F32, f"gate{t}")
+            nc.scalar.activation(gate[t][:], cv_banks[t][:], ACT.Sigmoid, scale=0.0625)
 
         y_rows = out_0.rearrange("(p t) c -> p t c", t=PACK)
         y_words = out_1[0].rearrange("p c r -> p (c r)").bitcast(I32)
@@ -224,15 +257,28 @@ def tile_picked_mombondgdif_none_po_kernel(
             cols = slice(first, first + width)
             entries = slice(first // 16, (first + width) // 16)
             y = tile([P, PACK, width], F32, f"y{first}")
+            diffs = tile([P, PACK, width], F32, f"diffs{first}")
+            fetched = tile([P, 2, width], F32, f"fetched{first}")
+
+            def gate_difference(t):
+                nc.vector.tensor_tensor(y[:, t, :], gate[t][:].indirect(n4_t[:, entries]), diffs[:, t, :], ALU.mult)
+
             for t in range(PACK):
+                if first == 0 and t != 1:
+                    empty_bank(t)
+                if first == 0 and t == 0:
+                    empty_bank(1)
+                if t < 2:
+                    nc.scalar.activation(fetched[:, t, :], cv[t][:].indirect(n4_t[:, entries]), ACT.Sigmoid)
                 other = tile([P, width], F32, f"other{first}_{t}")
-                gate = tile([P, width], F32, f"gate{first}_{t}")
-                diff = tile([P, width], F32, f"diff{first}_{t}")
-                fetches = [(other, n3_t, ACT.Copy), (gate, n4_t, ACT.Sigmoid)]
-                for fetched, lst, func in fetches[::-1] if first == 0 else fetches:
-                    nc.scalar.activation(fetched[:], cv[t][:].indirect(lst[:, entries]), func)
-                nc.vector.tensor_tensor(diff[:], cv[t][:, cols], other[:], ALU.subtract)
-                nc.vector.tensor_tensor(y[:, t, :], diff[:], gate[:], ALU.mult)
+                nc.scalar.activation(other[:], cv[t][:].indirect(n3_t[:, entries]), ACT.Copy)
+                if first == 0 and t >= 2:
+                    make_gate(t)
+                nc.vector.tensor_tensor(diffs[:, t, :], cv[t][:, cols], other[:], ALU.subtract)
+                if t == 2:
+                    nc.vector.tensor_tensor(y[:, :2, :], diffs[:, :2, :], fetched[:], ALU.mult)
+            gate_difference(2)
+            gate_difference(3)
             nc.sync.dma_start(y_rows[:, :, cols], y[:])
             y_g = tile([P, width, PACK], BF16, f"y_g{first}")
             interleave(nc.vector.tensor_copy, y_g[:], y[:])

@@ -62,21 +62,20 @@ def tile_picked_mombondgdif_none_po_kernel(
         nc.gpsimd.memset(xs[:].bitcast(I32), 0)
         offs_t = load_list(offs, "offs_t")
         two_t = load_list(two, "two_t")
-        wa_rows = wa.rearrange("(p j) c -> p j c", j=PACK)
-        wa_cols = [slice(0, 256), slice(256, 384), slice(384, 512)]
-        wa_raw = [tile([P, PACK, c.stop - c.start], F32, f"wa_raw{c.start}", tag="a_rows" if c.stop == H else "") for c in wa_cols]
-        nc.sync.dma_start(wa_raw[0][:], wa_rows[:, :, wa_cols[0]])
+        n1_t = load_list(n1, "n1_t")
         xs_rows = x_scales[0].bitcast(I32)
         for q in range(4):
             nc.sync.dma_start(xs[32 * q : 32 * q + 4, :].bitcast(I32), xs_rows[4 * q : 4 * q + 4, :])
         xw = tile([P, T], U32, "xw")
         nc.sync.dma_start(xw[:].bitcast(I32), x_words[0].rearrange("p c r -> p (c r)").bitcast(I32))
-        for i in (1, 2):
-            nc.sync.dma_start(wa_raw[i][:], wa_rows[:, :, wa_cols[i]])
-        n1_t = load_list(n1, "n1_t")
+        wa_rows = wa.rearrange("(p j) c -> p j c", j=PACK)
+        wa_cols = [slice(0, 256), slice(256, 384), slice(384, 512)]
+        wa_raw = [tile([P, PACK, c.stop - c.start], F32, f"wa_raw{c.start}", tag="a_rows" if c.stop == H else "") for c in wa_cols]
+        for raw, cols in zip(wa_raw, wa_cols):
+            nc.sync.dma_start(raw[:], wa_rows[:, :, cols])
         n2_t = load_list(n2, "n2_t")
         wb_rows = wb.rearrange("(p j) c -> p j c", j=PACK)
-        wb_raw = [tile([P, PACK, HALF], F32, f"wb_raw{h}", tag="" if h else "wb_first") for h in range(2)]
+        wb_raw = [tile([P, PACK, HALF], F32, f"wb_raw{h}") for h in range(2)]
         for h in range(2):
             nc.sync.dma_start(wb_raw[h][:], wb_rows[:, :, HALF * h : HALF * (h + 1)])
         identity = tile([P, P], F32, "identity")
@@ -119,6 +118,7 @@ def tile_picked_mombondgdif_none_po_kernel(
         xa_s = pick_scales(offs_t, "xa_s", tag="xa_s")
         xb_s = pick_scales(two_t, "xb_s")
         xa_w = pick_words(offs_t, "xa_w")
+        xb_w = pick_words(two_t, "xb_w")
 
         wa_q = tile([P, H], U32, "wa_q")
         wa_s = tile([P, H], U8, "wa_s")
@@ -134,17 +134,16 @@ def tile_picked_mombondgdif_none_po_kernel(
         for t in range(1, PACK):
             product(a_banks[t][:], xa_w, xa_s, t, wa_q[:], wa_s[:])
 
-        xb_w = pick_words(two_t, "xb_w", tag="wa_last")
-        wb_g = [tile([P, HALF, PACK], BF16, f"wb_g{h}", tag="" if h else "xa_s") for h in range(2)]
+        wb_g = [tile([P, HALF, PACK], BF16, f"wb_g{h}", tag="" if h else "wa_last") for h in range(2)]
         wb_q = tile([P, N], U32, "wb_q")
         wb_s = tile([P, N], U8, "wb_s")
-        interleave(nc.scalar.copy, wb_g[0][:], wb_raw[0][:])
-        interleave(nc.vector.tensor_copy, wb_g[1][:], wb_raw[1][:])
+        for h in range(2):
+            interleave(nc.vector.tensor_copy, wb_g[h][:], wb_raw[h][:])
 
         pa, pb, dt = [], [], []
         for t in range(PACK):
             if t > 0:
-                a_sb.append(tile([P, H], F32, f"a_sb{t}", tag="wb_first" if t == 2 else "a_rows"))
+                a_sb.append(tile([P, H], F32, f"a_sb{t}", tag="xa_s" if t == 2 else "a_rows"))
             a_t = a_sb[t]
             rest = slice(HALF if t == 0 else 0, H)
             nc.scalar.copy(a_t[:, rest], a_banks[t][:, rest])
@@ -159,7 +158,7 @@ def tile_picked_mombondgdif_none_po_kernel(
         gi_t = turn_weights(weight_rows[0], "gi_t", "first3")
 
         def put_sum(t):
-            dt.append(tile([P, H], F32, f"dt{t}"))
+            dt.append(tile([P, H], F32, f"dt{t}", tag="a_rows" if t == 2 else ""))
             nc.vector.tensor_tensor(dt[t][:].indirect(n1_t[:]), pa[t][:], pb[t][:], ALU.add)
 
         def put_product(t):
@@ -201,9 +200,9 @@ def tile_picked_mombondgdif_none_po_kernel(
         put_sum(1)
         put_product(0)
         weigh_z(0)
-        put_sum(2)
         put_product(1)
         weigh_z(1)
+        put_sum(2)
         put_sum(3)
         put_product(2)
         weigh_z(2)
@@ -239,7 +238,7 @@ def tile_picked_mombondgdif_none_po_kernel(
             if t == 0:
                 nc.vector.tensor_scalar(cv[t][:, :HALF], cv_early[:], 0.0625, None, ALU.mult)
                 nc.vector.tensor_scalar(cv[t][:, HALF:], cv_banks[t][:, HALF:], 0.0625, None, ALU.mult)
-            elif t < PACK - 1:
+            elif t == 1:
                 nc.vector.tensor_scalar(cv[t][:], cv_banks[t][:], 0.0625, None, ALU.mult)
             else:
                 nc.scalar.activation(cv[t][:], cv_banks[t][:], ACT.Copy, scale=0.0625)
@@ -263,7 +262,11 @@ def tile_picked_mombondgdif_none_po_kernel(
             def gate_difference(t):
                 nc.vector.tensor_tensor(y[:, t, :], gate[t][:].indirect(n4_t[:, entries]), diffs[:, t, :], ALU.mult)
 
-            for t in range(PACK):
+            def gate_first_pair():
+                nc.vector.tensor_tensor(y[:, :2, :], diffs[:, :2, :], fetched[:], ALU.mult)
+
+            order = [0, 1, 2, 3] if first == 0 else [2, 3, 0, 1]
+            for t in order:
                 if first == 0 and t != 1:
                     empty_bank(t)
                 if first == 0 and t == 0:
@@ -275,10 +278,13 @@ def tile_picked_mombondgdif_none_po_kernel(
                 if first == 0 and t >= 2:
                     make_gate(t)
                 nc.vector.tensor_tensor(diffs[:, t, :], cv[t][:, cols], other[:], ALU.subtract)
-                if t == 2:
-                    nc.vector.tensor_tensor(y[:, :2, :], diffs[:, :2, :], fetched[:], ALU.mult)
-            gate_difference(2)
-            gate_difference(3)
+                if first == 0 and t == 2:
+                    gate_first_pair()
+                if t == 3:
+                    gate_difference(2)
+                    gate_difference(3)
+            if first > 0:
+                gate_first_pair()
             nc.sync.dma_start(y_rows[:, :, cols], y[:])
             y_g = tile([P, width, PACK], BF16, f"y_g{first}")
             interleave(nc.vector.tensor_copy, y_g[:], y[:])

@@ -238,7 +238,7 @@ def tile_picked_mombondgdif_none_po_kernel(
             if t == 0:
                 nc.vector.tensor_scalar(cv[t][:, :HALF], cv_early[:], 0.0625, None, ALU.mult)
                 nc.vector.tensor_scalar(cv[t][:, HALF:], cv_banks[t][:, HALF:], 0.0625, None, ALU.mult)
-            elif t == 1:
+            elif t < PACK - 1:
                 nc.vector.tensor_scalar(cv[t][:], cv_banks[t][:], 0.0625, None, ALU.mult)
             else:
                 nc.scalar.activation(cv[t][:], cv_banks[t][:], ACT.Copy, scale=0.0625)

@@ -17,8 +17,16 @@ ALU = mybir.AluOpType
 ACT = mybir.ActivationFunctionType
 
 P = 128
-PACK = 4
+PLANES = 4
+RUN = 8
+QUADRANTS = 4
+LIST_ROWS = 16
 HALF = 256
+CV_SCALE = 0.0625
+
+WA_PIECES = (slice(0, 256), slice(256, 384), slice(384, 512))
+Z2_SCALAR_COLS = 384
+OUT_PIECES = ((0, 256, 2), (256, 128, 2), (384, 128, 3))
 
 
 def tile_picked_mombondgdif_none_po_kernel(
@@ -33,14 +41,20 @@ def tile_picked_mombondgdif_none_po_kernel(
             return sb.tile(shape, dtype, name=name, tag=tag, align_bytes=64)
 
         def load_list(src, name):
-            t = tile([P, src.shape[1]], U16, name)
-            nc.sync.dma_start(t[:], src)
-            return t
+            offsets = tile([P, src.shape[1]], U16, name)
+            nc.sync.dma_start(offsets[:], src)
+            return offsets
 
         def interleave(copy, grouped, planes):
             copy(
                 out=grouped.rearrange("p (c i) t -> p c t i", i=4),
                 in_=planes.rearrange("p t (c i) -> p c t i", i=4),
+            )
+
+        def merge_pairs(copy, word, grouped, pairs):
+            copy(
+                grouped.bitcast(word).rearrange("p (c i u) -> p c u i", i=2, u=2),
+                pairs.rearrange("p u c e -> p u (c e)").bitcast(word).rearrange("p u (c i) -> p c u i", i=2),
             )
 
         def quantize(codes, scales, grouped):
@@ -64,55 +78,60 @@ def tile_picked_mombondgdif_none_po_kernel(
         two_t = load_list(two, "two_t")
         n1_t = load_list(n1, "n1_t")
         xs_rows = x_scales[0].bitcast(I32)
-        for q in range(4):
+        for q in range(QUADRANTS):
             nc.sync.dma_start(xs[32 * q : 32 * q + 4, :].bitcast(I32), xs_rows[4 * q : 4 * q + 4, :])
         xw = tile([P, T], U32, "xw")
         nc.sync.dma_start(xw[:].bitcast(I32), x_words[0].rearrange("p c r -> p (c r)").bitcast(I32))
-        wa_rows = wa.rearrange("(p j) c -> p j c", j=PACK)
-        wa_cols = [slice(0, 256), slice(256, 384), slice(384, 512)]
-        wa_raw = [tile([P, PACK, c.stop - c.start], F32, f"wa_raw{c.start}", tag="a_rows" if c.stop == H else "") for c in wa_cols]
-        for raw, cols in zip(wa_raw, wa_cols):
+        wa_rows = wa.rearrange("(p j) c -> p j c", j=PLANES)
+        wa_raw = [
+            tile([P, PLANES, c.stop - c.start], F32, f"wa_raw{c.start}", tag="a_rows" if c.stop == H else "")
+            for c in WA_PIECES
+        ]
+        for raw, cols in zip(wa_raw, WA_PIECES):
             nc.sync.dma_start(raw[:], wa_rows[:, :, cols])
         n2_t = load_list(n2, "n2_t")
-        wb_rows = wb.rearrange("(p j) c -> p j c", j=PACK)
-        wb_raw = [tile([P, PACK, HALF], F32, f"wb_raw{h}") for h in range(2)]
+        wb_rows = wb.rearrange("(p j) c -> p j c", j=PLANES)
+        wb_raw = [tile([P, PLANES, HALF], F32, f"wb_raw{h}") for h in range(2)]
         for h in range(2):
             nc.sync.dma_start(wb_raw[h][:], wb_rows[:, :, HALF * h : HALF * (h + 1)])
+
         identity = tile([P, P], F32, "identity")
         make_identity(nc, identity[:])
-        weight_rows = []
+        weight_rows = {}
         for name, src in (("gi_rows", gi), ("gt_rows", gt)):
             rows = tile([P, P], F32, name)
             nc.gpsimd.memset(rows[:], 0.0)
             nc.sync.dma_start(
-                rows[:PACK, :].rearrange("t (q r) -> t q r", r=8),
-                src.rearrange("(q t r) o -> t q (r o)", t=PACK, r=8),
+                rows[:PLANES, :].rearrange("t (q r) -> t q r", r=RUN),
+                src.rearrange("(q t r) o -> t q (r o)", t=PLANES, r=RUN),
             )
-            weight_rows.append(rows)
+            weight_rows[name] = rows
 
         def turn_weights(rows, name, tag):
             turned = ps.tile([P, P], F32, name=name + "_turned", tag=tag)
             nc.tensor.transpose(turned[:], rows[:], identity[:])
-            weights = tile([P, PACK], F32, name)
-            nc.scalar.copy(weights[:], turned[:, :PACK])
+            weights = tile([P, PLANES], F32, name)
+            nc.scalar.copy(weights[:], turned[:, :PLANES])
             return weights
 
         n3_t = load_list(n3, "n3_t")
         n4_t = load_list(n4, "n4_t")
 
-        def pick_scales(lst, name, tag=""):
+        def pick_scales(offsets, name, tag=""):
             picked = tile([P, S], U8, name + "_picked")
-            nc.vector.tensor_copy(picked[:], xs[:].indirect(lst[:]))
+            nc.vector.tensor_copy(picked[:], xs[:].indirect(offsets[:]))
             dealt = tile([P, S], U8, name + "_dealt", tag=tag)
             nc.vector.tensor_copy(
-                dealt[:].bitcast(I32).rearrange("p (t q w) -> p q t w", t=PACK, w=2),
-                picked[:].bitcast(I32).rearrange("p (q t w) -> p q t w", t=PACK, w=2),
+                dealt[:].bitcast(I32).rearrange("p (t q w) -> p q t w", t=PLANES, w=2),
+                picked[:].bitcast(I32).rearrange("p (q t w) -> p q t w", t=PLANES, w=2),
             )
             return dealt
 
-        def pick_words(lst, name, tag=""):
-            picked = tile([P, S], U32, name, tag=tag)
-            nc.vector.tensor_copy(picked[:].rearrange("p (t q r) -> p q t r", t=PACK, r=8), xw[:].indirect(lst[:]))
+        def pick_words(offsets, name):
+            picked = tile([P, S], U32, name)
+            nc.vector.tensor_copy(
+                picked[:].rearrange("p (t q r) -> p q t r", t=PLANES, r=RUN), xw[:].indirect(offsets[:])
+            )
             return picked
 
         xa_s = pick_scales(offs_t, "xa_s", tag="xa_s")
@@ -122,40 +141,39 @@ def tile_picked_mombondgdif_none_po_kernel(
 
         wa_q = tile([P, H], U32, "wa_q")
         wa_s = tile([P, H], U8, "wa_s")
-        a_banks = [ps.tile([P, H], F32, name=f"a{t}", tag=f"first{t}") for t in range(PACK)]
+        a_banks = [ps.tile([P, H], F32, name=f"a{t}", tag=f"first{t}") for t in range(PLANES)]
         a_early = ps.tile([P, HALF], F32, name="a_early", tag="second0")
-        for i, cols in enumerate(wa_cols):
-            wa_g = tile([P, cols.stop - cols.start, PACK], BF16, f"wa_g{i}", tag="wa_last" if i == 2 else "")
+        for i, cols in enumerate(WA_PIECES):
+            wa_g = tile([P, cols.stop - cols.start, PLANES], BF16, f"wa_g{i}", tag="wa_last" if cols.stop == H else "")
             interleave(nc.scalar.copy, wa_g[:], wa_raw[i][:])
             quantize(wa_q[:, cols], wa_s[:, cols], wa_g[:].rearrange("p c t -> p (c t)"))
             product(a_early[:] if i == 0 else a_banks[0][:, cols], xa_w, xa_s, 0, wa_q[:, cols], wa_s[:, cols])
         a_sb = [tile([P, H], F32, "a_sb0", tag="a_rows")]
         nc.scalar.copy(a_sb[0][:, :HALF], a_early[:])
-        for t in range(1, PACK):
+        for t in range(1, PLANES):
             product(a_banks[t][:], xa_w, xa_s, t, wa_q[:], wa_s[:])
 
-        wb_g = [tile([P, HALF, PACK], BF16, f"wb_g{h}", tag="" if h else "wa_last") for h in range(2)]
+        wb_g = [tile([P, HALF, PLANES], BF16, f"wb_g{h}", tag="" if h else "wa_last") for h in range(2)]
         wb_q = tile([P, N], U32, "wb_q")
         wb_s = tile([P, N], U8, "wb_s")
         for h in range(2):
             interleave(nc.vector.tensor_copy, wb_g[h][:], wb_raw[h][:])
 
         pa, pb, dt = [], [], []
-        for t in range(PACK):
+        for t in range(PLANES):
             if t > 0:
                 a_sb.append(tile([P, H], F32, f"a_sb{t}", tag="xa_s" if t == 2 else "a_rows"))
-            a_t = a_sb[t]
             rest = slice(HALF if t == 0 else 0, H)
-            nc.scalar.copy(a_t[:, rest], a_banks[t][:, rest])
+            nc.scalar.copy(a_sb[t][:, rest], a_banks[t][:, rest])
             pa.append(tile([P, W], F32, f"pa{t}"))
             pb.append(tile([P, W], F32, f"pb{t}"))
-            nc.scalar.activation(pa[t][:], a_t[:].indirect(n1_t[:]), ACT.Copy)
+            nc.scalar.activation(pa[t][:], a_sb[t][:].indirect(n1_t[:]), ACT.Copy)
             if t == 0:
-                nc.vector.tensor_copy(pb[t][:], a_t[:].indirect(n2_t[:]))
+                nc.vector.tensor_copy(pb[t][:], a_sb[t][:].indirect(n2_t[:]))
             else:
-                nc.scalar.activation(pb[t][:], a_t[:].indirect(n2_t[:]), ACT.Copy)
+                nc.scalar.activation(pb[t][:], a_sb[t][:].indirect(n2_t[:]), ACT.Copy)
 
-        gi_t = turn_weights(weight_rows[0], "gi_t", "first3")
+        gi_t = turn_weights(weight_rows["gi_rows"], "gi_t", "first3")
 
         def put_sum(t):
             dt.append(tile([P, H], F32, f"dt{t}", tag="a_rows" if t == 2 else ""))
@@ -165,22 +183,17 @@ def tile_picked_mombondgdif_none_po_kernel(
             nc.vector.tensor_tensor(dt[t][:].indirect(n2_t[:]), pa[t][:], pb[t][:], ALU.mult)
 
         put_sum(0)
+
         for h in range(2):
             cols = slice(HALF * h, HALF * (h + 1))
             quantize(wb_q[:, cols], wb_s[:, cols], wb_g[h][:].rearrange("p c t -> p (c t)"))
-        b_banks = [ps.tile([P, N], F32, name=f"b{t}", tag=f"second{t}") for t in range(PACK)]
-        for t in range(PACK):
+        b_banks = [ps.tile([P, N], F32, name=f"b{t}", tag=f"second{t}") for t in range(PLANES)]
+        for t in range(PLANES):
             product(b_banks[t][:], xb_w, xb_s, t, wb_q[:], wb_s[:])
         z2_pairs = tile([P, 2, N, 2], BF16, "z2_pairs")
-        for t in range(PACK):
+        for t in range(PLANES):
             nc.scalar.activation(z2_pairs[:, t // 2, :, t % 2], b_banks[t][:], ACT.Copy, scale=gi_t[:, t : t + 1])
-        gt_t = turn_weights(weight_rows[1], "gt_t", "second3")
-
-        def merge_pairs(copy, word, grouped, pairs):
-            copy(
-                grouped.bitcast(word).rearrange("p (c i u) -> p c u i", i=2, u=2),
-                pairs.rearrange("p u c e -> p u (c e)").bitcast(word).rearrange("p u (c i) -> p c u i", i=2),
-            )
+        gt_t = turn_weights(weight_rows["gt_rows"], "gt_t", "second3")
 
         z_pairs = [tile([P, 2, HALF, 2], BF16, f"z_pairs{h}") for h in range(2)]
 
@@ -188,24 +201,24 @@ def tile_picked_mombondgdif_none_po_kernel(
             for h in range(2):
                 nc.scalar.activation(
                     z_pairs[h][:, t // 2, :, t % 2].rearrange("p (a m) -> p m a", a=2),
-                    dt[t][:].rearrange("p (m a) -> p m a", a=PACK)[:, :, 2 * h : 2 * h + 2],
+                    dt[t][:].rearrange("p (m a) -> p m a", a=PLANES)[:, :, 2 * h : 2 * h + 2],
                     ACT.Copy,
                     scale=gt_t[:, t : t + 1],
                 )
 
-        z2_g = tile([P, N * PACK], BF16, "z2_g")
+        z2_g = tile([P, N * PLANES], BF16, "z2_g")
         z2_q = tile([P, N], U32, "z2_q")
         z2_s = tile([P, N], U8, "z2_s")
-        merge_pairs(nc.scalar.copy, U32, z2_g[:], z2_pairs[:])
+        merge_pairs(nc.scalar.copy, U32, z2_g[:, : Z2_SCALAR_COLS * PLANES], z2_pairs[:, :, :Z2_SCALAR_COLS, :])
         put_sum(1)
-        put_product(0)
-        weigh_z(0)
-        put_product(1)
-        weigh_z(1)
+        for t in (0, 1):
+            put_product(t)
+            weigh_z(t)
         put_sum(2)
         put_sum(3)
         put_product(2)
         weigh_z(2)
+        merge_pairs(nc.vector.tensor_copy, I32, z2_g[:, Z2_SCALAR_COLS * PLANES :], z2_pairs[:, :, Z2_SCALAR_COLS:, :])
         put_product(3)
         quantize(z2_q[:], z2_s[:], z2_g[:])
         weigh_z(3)
@@ -213,9 +226,8 @@ def tile_picked_mombondgdif_none_po_kernel(
         z_q = tile([P, H], U32, "z_q")
         z_s = tile([P, H], U8, "z_s")
         cv, gate = [], {}
-        cv_banks = [ps.tile([P, N], F32, name=f"cv{t}", tag=f"first{t}") for t in range(PACK)]
-        z_g = [tile([P, P * PACK], BF16, f"z_g{t}") for t in range(PACK)]
-
+        cv_banks = [ps.tile([P, N], F32, name=f"cv{t}", tag=f"first{t}") for t in range(PLANES)]
+        z_g = [tile([P, P * PLANES], BF16, f"z_g{t}") for t in range(PLANES)]
         cv_early = ps.tile([P, HALF], F32, name="cv_early", tag="second0")
 
         def finish_z(t):
@@ -227,69 +239,80 @@ def tile_picked_mombondgdif_none_po_kernel(
             else:
                 product(cv_banks[t][:], z_q, z_s, t, z2_q[:], z2_s[:])
 
-        for t in range(PACK):
+        for t in range(PLANES):
             merge_pairs(nc.vector.tensor_copy, I32, z_g[t][:], z_pairs[t // 2][:, :, P * (t % 2) : P * (t % 2 + 1), :])
             if t > 0:
                 finish_z(t - 1)
-        finish_z(PACK - 1)
+        finish_z(PLANES - 1)
 
         def empty_bank(t):
             cv.append(tile([P, N], F32, f"cv_sb{t}"))
             if t == 0:
-                nc.vector.tensor_scalar(cv[t][:, :HALF], cv_early[:], 0.0625, None, ALU.mult)
-                nc.vector.tensor_scalar(cv[t][:, HALF:], cv_banks[t][:, HALF:], 0.0625, None, ALU.mult)
-            elif t < PACK - 1:
-                nc.vector.tensor_scalar(cv[t][:], cv_banks[t][:], 0.0625, None, ALU.mult)
+                nc.vector.tensor_scalar(cv[t][:, :HALF], cv_early[:], CV_SCALE, None, ALU.mult)
+                nc.vector.tensor_scalar(cv[t][:, HALF:], cv_banks[t][:, HALF:], CV_SCALE, None, ALU.mult)
+            elif t < PLANES - 1:
+                nc.vector.tensor_scalar(cv[t][:], cv_banks[t][:], CV_SCALE, None, ALU.mult)
             else:
-                nc.scalar.activation(cv[t][:], cv_banks[t][:], ACT.Copy, scale=0.0625)
+                nc.scalar.activation(cv[t][:], cv_banks[t][:], ACT.Copy, scale=CV_SCALE)
 
         def make_gate(t):
             gate[t] = tile([P, N], F32, f"gate{t}")
-            nc.scalar.activation(gate[t][:], cv_banks[t][:], ACT.Sigmoid, scale=0.0625)
+            nc.scalar.activation(gate[t][:], cv_banks[t][:], ACT.Sigmoid, scale=CV_SCALE)
 
-        y_rows = out_0.rearrange("(p t) c -> p t c", t=PACK)
+        y_rows = out_0.rearrange("(p t) c -> p t c", t=PLANES)
         y_words = out_1[0].rearrange("p c r -> p (c r)").bitcast(I32)
         y_scales = out_2[0].bitcast(I32)
         y_q = tile([P, N], U32, "y_q")
         y_s = tile([P, N], U8, "y_s")
-        for first, width in ((0, 256), (256, 128), (384, 128)):
+        for first, width, direct in OUT_PIECES:
             cols = slice(first, first + width)
-            entries = slice(first // 16, (first + width) // 16)
-            y = tile([P, PACK, width], F32, f"y{first}")
-            diffs = tile([P, PACK, width], F32, f"diffs{first}")
-            fetched = tile([P, 2, width], F32, f"fetched{first}")
+            entries = slice(first // LIST_ROWS, (first + width) // LIST_ROWS)
+            y = tile([P, PLANES, width], F32, f"y{first}")
+            diffs = tile([P, PLANES, width], F32, f"diffs{first}")
+            fetched = tile([P, direct, width], F32, f"fetched{first}")
 
-            def gate_difference(t):
-                nc.vector.tensor_tensor(y[:, t, :], gate[t][:].indirect(n4_t[:, entries]), diffs[:, t, :], ALU.mult)
+            def fetch_gate(t):
+                nc.scalar.activation(fetched[:, t, :], cv[t][:].indirect(n4_t[:, entries]), ACT.Sigmoid)
 
-            def gate_first_pair():
-                nc.vector.tensor_tensor(y[:, :2, :], diffs[:, :2, :], fetched[:], ALU.mult)
-
-            order = [0, 1, 2, 3] if first == 0 else [2, 3, 0, 1]
-            for t in order:
-                if first == 0 and t != 1:
-                    empty_bank(t)
-                if first == 0 and t == 0:
-                    empty_bank(1)
-                if t < 2:
-                    nc.scalar.activation(fetched[:, t, :], cv[t][:].indirect(n4_t[:, entries]), ACT.Sigmoid)
+            def subtract_other(t):
                 other = tile([P, width], F32, f"other{first}_{t}")
                 nc.scalar.activation(other[:], cv[t][:].indirect(n3_t[:, entries]), ACT.Copy)
-                if first == 0 and t >= 2:
+                if first == 0 and t >= direct:
                     make_gate(t)
                 nc.vector.tensor_tensor(diffs[:, t, :], cv[t][:, cols], other[:], ALU.subtract)
-                if first == 0 and t == 2:
-                    gate_first_pair()
-                if t == 3:
-                    gate_difference(2)
-                    gate_difference(3)
-            if first > 0:
-                gate_first_pair()
+
+            def apply_fetched(planes):
+                nc.vector.tensor_tensor(y[:, planes, :], diffs[:, planes, :], fetched[:, planes, :], ALU.mult)
+
+            def apply_gates():
+                for t in range(direct, PLANES):
+                    nc.vector.tensor_tensor(y[:, t, :], gate[t][:].indirect(n4_t[:, entries]), diffs[:, t, :], ALU.mult)
+
+            if first == 0:
+                empty_bank(0)
+                empty_bank(1)
+                for t in range(PLANES):
+                    if t > 1:
+                        empty_bank(t)
+                    if t < direct:
+                        fetch_gate(t)
+                    subtract_other(t)
+                    if t == direct:
+                        apply_fetched(slice(0, direct))
+                apply_gates()
+            else:
+                for t in list(range(direct, PLANES)) + list(range(direct)):
+                    subtract_other(t)
+                apply_gates()
+                for t in range(direct):
+                    fetch_gate(t)
+                apply_fetched(slice(0, direct - 1))
+                apply_fetched(slice(direct - 1, direct))
             nc.sync.dma_start(y_rows[:, :, cols], y[:])
-            y_g = tile([P, width, PACK], BF16, f"y_g{first}")
+            y_g = tile([P, width, PLANES], BF16, f"y_g{first}")
             interleave(nc.vector.tensor_copy, y_g[:], y[:])
             quantize(y_q[:, cols], y_s[:, cols], y_g[:].rearrange("p c t -> p (c t)"))
             nc.sync.dma_start(y_words[:, cols], y_q[:, cols].bitcast(I32))
-        for q in range(4):
+        for q in range(QUADRANTS):
             queue = nc.scalar if q % 2 else nc.sync
             queue.dma_start(y_scales[4 * q : 4 * q + 4, :], y_s[32 * q : 32 * q + 4, :].bitcast(I32))

from contextlib import ExitStack

import concourse.mybir as mybir
from concourse.masks import make_identity

K, T, S, N, H, W = 512, 2048, 512, 512, 512, 256
FLOPS = 2 * (K * S * H + K * S * N + S * H * N)

F32 = mybir.dt.float32
BF16 = mybir.dt.bfloat16
I32 = mybir.dt.int32
U32 = mybir.dt.uint32
U16 = mybir.dt.uint16
U8 = mybir.dt.uint8
FP8X4 = mybir.dt.float8_e4m3fn_x4
ALU = mybir.AluOpType
ACT = mybir.ActivationFunctionType

P = 128
PLANES = 4
RUN = 8
QUADRANTS = 4
LIST_ROWS = 16
HALF = 256
CV_SCALE = 0.0625

WA_PIECES = (slice(0, 256), slice(256, 384), slice(384, 512))
Z2_SCALAR_COLS = 384
OUT_PIECES = ((0, 256, 2), (256, 128, 2), (384, 128, 3))


def tile_picked_mombondgdif_none_po_kernel(
    tc, x_words, x_scales, wa, wb, gt, gi, offs, two, n1, n2, n3, n4, out_0, out_1, out_2
):
    nc = tc.nc
    with ExitStack() as ctx:
        sb = ctx.enter_context(tc.tile_pool(name="sb", bufs=1))
        ps = ctx.enter_context(tc.psum_pool(name="ps", bufs=1))

        def tile(shape, dtype, name, tag=""):
            return sb.tile(shape, dtype, name=name, tag=tag, align_bytes=64)

        def load_list(src, name):
            offsets = tile([P, src.shape[1]], U16, name)
            nc.sync.dma_start(offsets[:], src)
            return offsets

        def interleave(copy, grouped, planes):
            copy(
                out=grouped.rearrange("p (c i) t -> p c t i", i=4),
                in_=planes.rearrange("p t (c i) -> p c t i", i=4),
            )

        def merge_pairs(copy, word, grouped, pairs):
            copy(
                grouped.bitcast(word).rearrange("p (c i u) -> p c u i", i=2, u=2),
                pairs.rearrange("p u c e -> p u (c e)").bitcast(word).rearrange("p u (c i) -> p c u i", i=2),
            )

        def quantize(codes, scales, grouped):
            nc.vector.quantize_mx(out=codes.bitcast(FP8X4), scales=scales, in_=grouped)

        def product(bank, lhs_codes, lhs_scales, t, rhs_codes, rhs_scales):
            cols = slice(P * t, P * (t + 1))
            nc.tensor.matmul_mx(
                out=bank,
                lhsT=lhs_codes[:, cols].bitcast(FP8X4),
                lhsT_scale=lhs_scales[:, cols],
                rhs=rhs_codes.bitcast(FP8X4),
                rhs_scale=rhs_scales,
                start=True,
                stop=True,
            )

        xs = tile([P, T], U8, "xs")
        nc.gpsimd.memset(xs[:].bitcast(I32), 0)
        offs_t = load_list(offs, "offs_t")
        two_t = load_list(two, "two_t")
        n1_t = load_list(n1, "n1_t")
        xs_rows = x_scales[0].bitcast(I32)
        for q in range(QUADRANTS):
            nc.sync.dma_start(xs[32 * q : 32 * q + 4, :].bitcast(I32), xs_rows[4 * q : 4 * q + 4, :])
        xw = tile([P, T], U32, "xw")
        nc.sync.dma_start(xw[:].bitcast(I32), x_words[0].rearrange("p c r -> p (c r)").bitcast(I32))
        wa_rows = wa.rearrange("(p j) c -> p j c", j=PLANES)
        wa_raw = [
            tile([P, PLANES, c.stop - c.start], F32, f"wa_raw{c.start}", tag="a_rows" if c.stop == H else "")
            for c in WA_PIECES
        ]
        for raw, cols in zip(wa_raw, WA_PIECES):
            nc.sync.dma_start(raw[:], wa_rows[:, :, cols])
        n2_t = load_list(n2, "n2_t")
        wb_rows = wb.rearrange("(p j) c -> p j c", j=PLANES)
        wb_raw = [tile([P, PLANES, HALF], F32, f"wb_raw{h}") for h in range(2)]
        for h in range(2):
            nc.sync.dma_start(wb_raw[h][:], wb_rows[:, :, HALF * h : HALF * (h + 1)])

        identity = tile([P, P], F32, "identity")
        make_identity(nc, identity[:])
        weight_rows = {}
        for name, src in (("gi_rows", gi), ("gt_rows", gt)):
            rows = tile([P, P], F32, name)
            nc.gpsimd.memset(rows[:], 0.0)
            nc.sync.dma_start(
                rows[:PLANES, :].rearrange("t (q r) -> t q r", r=RUN),
                src.rearrange("(q t r) o -> t q (r o)", t=PLANES, r=RUN),
            )
            weight_rows[name] = rows

        def turn_weights(rows, name, tag):
            turned = ps.tile([P, P], F32, name=name + "_turned", tag=tag)
            nc.tensor.transpose(turned[:], rows[:], identity[:])
            weights = tile([P, PLANES], F32, name)
            nc.scalar.copy(weights[:], turned[:, :PLANES])
            return weights

        n3_t = load_list(n3, "n3_t")
        n4_t = load_list(n4, "n4_t")

        def pick_scales(offsets, name, tag=""):
            picked = tile([P, S], U8, name + "_picked")
            nc.vector.tensor_copy(picked[:], xs[:].indirect(offsets[:]))
            dealt = tile([P, S], U8, name + "_dealt", tag=tag)
            nc.vector.tensor_copy(
                dealt[:].bitcast(I32).rearrange("p (t q w) -> p q t w", t=PLANES, w=2),
                picked[:].bitcast(I32).rearrange("p (q t w) -> p q t w", t=PLANES, w=2),
            )
            return dealt

        def pick_words(offsets, name):
            picked = tile([P, S], U32, name)
            nc.vector.tensor_copy(
                picked[:].rearrange("p (t q r) -> p q t r", t=PLANES, r=RUN), xw[:].indirect(offsets[:])
            )
            return picked

        xa_s = pick_scales(offs_t, "xa_s", tag="xa_s")
        xb_s = pick_scales(two_t, "xb_s")
        xa_w = pick_words(offs_t, "xa_w")
        xb_w = pick_words(two_t, "xb_w")

        wa_q = tile([P, H], U32, "wa_q")
        wa_s = tile([P, H], U8, "wa_s")
        a_banks = [ps.tile([P, H], F32, name=f"a{t}", tag=f"first{t}") for t in range(PLANES)]
        a_early = ps.tile([P, HALF], F32, name="a_early", tag="second0")
        for i, cols in enumerate(WA_PIECES):
            wa_g = tile([P, cols.stop - cols.start, PLANES], BF16, f"wa_g{i}", tag="wa_last" if cols.stop == H else "")
            interleave(nc.scalar.copy, wa_g[:], wa_raw[i][:])
            quantize(wa_q[:, cols], wa_s[:, cols], wa_g[:].rearrange("p c t -> p (c t)"))
            product(a_early[:] if i == 0 else a_banks[0][:, cols], xa_w, xa_s, 0, wa_q[:, cols], wa_s[:, cols])
        a_sb = [tile([P, H], F32, "a_sb0", tag="a_rows")]
        nc.scalar.copy(a_sb[0][:, :HALF], a_early[:])
        for t in range(1, PLANES):
            product(a_banks[t][:], xa_w, xa_s, t, wa_q[:], wa_s[:])

        wb_g = [tile([P, HALF, PLANES], BF16, f"wb_g{h}", tag="" if h else "wa_last") for h in range(2)]
        wb_q = tile([P, N], U32, "wb_q")
        wb_s = tile([P, N], U8, "wb_s")
        for h in range(2):
            interleave(nc.vector.tensor_copy, wb_g[h][:], wb_raw[h][:])

        pa, pb, dt = [], [], []
        for t in range(PLANES):
            if t > 0:
                a_sb.append(tile([P, H], F32, f"a_sb{t}", tag="xa_s" if t == 2 else "a_rows"))
            rest = slice(HALF if t == 0 else 0, H)
            nc.scalar.copy(a_sb[t][:, rest], a_banks[t][:, rest])
            pa.append(tile([P, W], F32, f"pa{t}"))
            pb.append(tile([P, W], F32, f"pb{t}"))
            nc.scalar.activation(pa[t][:], a_sb[t][:].indirect(n1_t[:]), ACT.Copy)
            if t == 0:
                nc.vector.tensor_copy(pb[t][:], a_sb[t][:].indirect(n2_t[:]))
            else:
                nc.scalar.activation(pb[t][:], a_sb[t][:].indirect(n2_t[:]), ACT.Copy)

        gi_t = turn_weights(weight_rows["gi_rows"], "gi_t", "first3")

        def put_sum(t):
            dt.append(tile([P, H], F32, f"dt{t}", tag="a_rows" if t == 2 else ""))
            nc.vector.tensor_tensor(dt[t][:].indirect(n1_t[:]), pa[t][:], pb[t][:], ALU.add)

        def put_product(t):
            nc.vector.tensor_tensor(dt[t][:].indirect(n2_t[:]), pa[t][:], pb[t][:], ALU.mult)

        put_sum(0)

        for h in range(2):
            cols = slice(HALF * h, HALF * (h + 1))
            quantize(wb_q[:, cols], wb_s[:, cols], wb_g[h][:].rearrange("p c t -> p (c t)"))
        b_banks = [ps.tile([P, N], F32, name=f"b{t}", tag=f"second{t}") for t in range(PLANES)]
        for t in range(PLANES):
            product(b_banks[t][:], xb_w, xb_s, t, wb_q[:], wb_s[:])
        z2_pairs = tile([P, 2, N, 2], BF16, "z2_pairs")
        for t in range(PLANES):
            nc.scalar.activation(z2_pairs[:, t // 2, :, t % 2], b_banks[t][:], ACT.Copy, scale=gi_t[:, t : t + 1])
        gt_t = turn_weights(weight_rows["gt_rows"], "gt_t", "second3")

        z_pairs = [tile([P, 2, HALF, 2], BF16, f"z_pairs{h}") for h in range(2)]

        def weigh_z(t):
            for h in range(2):
                nc.scalar.activation(
                    z_pairs[h][:, t // 2, :, t % 2].rearrange("p (a m) -> p m a", a=2),
                    dt[t][:].rearrange("p (m a) -> p m a", a=PLANES)[:, :, 2 * h : 2 * h + 2],
                    ACT.Copy,
                    scale=gt_t[:, t : t + 1],
                )

        z2_g = tile([P, N * PLANES], BF16, "z2_g")
        z2_q = tile([P, N], U32, "z2_q")
        z2_s = tile([P, N], U8, "z2_s")
        merge_pairs(nc.scalar.copy, U32, z2_g[:, : Z2_SCALAR_COLS * PLANES], z2_pairs[:, :, :Z2_SCALAR_COLS, :])
        put_sum(1)
        for t in (0, 1):
            put_product(t)
            weigh_z(t)
        put_sum(2)
        put_sum(3)
        put_product(2)
        weigh_z(2)
        merge_pairs(nc.vector.tensor_copy, I32, z2_g[:, Z2_SCALAR_COLS * PLANES :], z2_pairs[:, :, Z2_SCALAR_COLS:, :])
        put_product(3)
        quantize(z2_q[:], z2_s[:], z2_g[:])
        weigh_z(3)

        z_q = tile([P, H], U32, "z_q")
        z_s = tile([P, H], U8, "z_s")
        cv, gate = [], {}
        cv_banks = [ps.tile([P, N], F32, name=f"cv{t}", tag=f"first{t}") for t in range(PLANES)]
        z_g = [tile([P, P * PLANES], BF16, f"z_g{t}") for t in range(PLANES)]
        cv_early = ps.tile([P, HALF], F32, name="cv_early", tag="second0")

        def finish_z(t):
            cols = slice(P * t, P * (t + 1))
            quantize(z_q[:, cols], z_s[:, cols], z_g[t][:])
            if t == 0:
                product(cv_early[:], z_q, z_s, t, z2_q[:, :HALF], z2_s[:, :HALF])
                product(cv_banks[t][:, HALF:], z_q, z_s, t, z2_q[:, HALF:], z2_s[:, HALF:])
            else:
                product(cv_banks[t][:], z_q, z_s, t, z2_q[:], z2_s[:])

        for t in range(PLANES):
            merge_pairs(nc.vector.tensor_copy, I32, z_g[t][:], z_pairs[t // 2][:, :, P * (t % 2) : P * (t % 2 + 1), :])
            if t > 0:
                finish_z(t - 1)
        finish_z(PLANES - 1)

        def empty_bank(t):
            cv.append(tile([P, N], F32, f"cv_sb{t}"))
            if t == 0:
                nc.vector.tensor_scalar(cv[t][:, :HALF], cv_early[:], CV_SCALE, None, ALU.mult)
                nc.vector.tensor_scalar(cv[t][:, HALF:], cv_banks[t][:, HALF:], CV_SCALE, None, ALU.mult)
            elif t < PLANES - 1:
                nc.vector.tensor_scalar(cv[t][:], cv_banks[t][:], CV_SCALE, None, ALU.mult)
            else:
                nc.scalar.activation(cv[t][:], cv_banks[t][:], ACT.Copy, scale=CV_SCALE)

        def make_gate(t):
            gate[t] = tile([P, N], F32, f"gate{t}")
            nc.scalar.activation(gate[t][:], cv_banks[t][:], ACT.Sigmoid, scale=CV_SCALE)

        y_rows = out_0.rearrange("(p t) c -> p t c", t=PLANES)
        y_words = out_1[0].rearrange("p c r -> p (c r)").bitcast(I32)
        y_scales = out_2[0].bitcast(I32)
        y_q = tile([P, N], U32, "y_q")
        y_s = tile([P, N], U8, "y_s")
        for first, width, direct in OUT_PIECES:
            cols = slice(first, first + width)
            entries = slice(first // LIST_ROWS, (first + width) // LIST_ROWS)
            y = tile([P, PLANES, width], F32, f"y{first}")
            diffs = tile([P, PLANES, width], F32, f"diffs{first}")
            fetched = tile([P, direct, width], F32, f"fetched{first}")

            def fetch_gate(t):
                nc.scalar.activation(fetched[:, t, :], cv[t][:].indirect(n4_t[:, entries]), ACT.Sigmoid)

            def subtract_other(t):
                other = tile([P, width], F32, f"other{first}_{t}")
                nc.scalar.activation(other[:], cv[t][:].indirect(n3_t[:, entries]), ACT.Copy)
                if first == 0 and t >= direct:
                    make_gate(t)
                nc.vector.tensor_tensor(diffs[:, t, :], cv[t][:, cols], other[:], ALU.subtract)

            def apply_fetched(planes):
                nc.vector.tensor_tensor(y[:, planes, :], diffs[:, planes, :], fetched[:, planes, :], ALU.mult)

            def apply_gates():
                for t in range(direct, PLANES):
                    nc.vector.tensor_tensor(y[:, t, :], gate[t][:].indirect(n4_t[:, entries]), diffs[:, t, :], ALU.mult)

            if first == 0:
                empty_bank(0)
                empty_bank(1)
                for t in range(PLANES):
                    if t > 1:
                        empty_bank(t)
                    if t < direct:
                        fetch_gate(t)
                    subtract_other(t)
                    if t == direct:
                        apply_fetched(slice(0, direct))
                apply_gates()
            else:
                for t in list(range(direct, PLANES)) + list(range(direct)):
                    subtract_other(t)
                apply_gates()
                for t in range(direct):
                    fetch_gate(t)
                apply_fetched(slice(0, direct - 1))
                apply_fetched(slice(direct - 1, direct))
            nc.sync.dma_start(y_rows[:, :, cols], y[:])
            y_g = tile([P, width, PLANES], BF16, f"y_g{first}")
            interleave(nc.vector.tensor_copy, y_g[:], y[:])
            quantize(y_q[:, cols], y_s[:, cols], y_g[:].rearrange("p c t -> p (c t)"))
            nc.sync.dma_start(y_words[:, cols], y_q[:, cols].bitcast(I32))
        for q in range(QUADRANTS):
            queue = nc.scalar if q % 2 else nc.sync
            queue.dma_start(y_scales[4 * q : 4 * q + 4, :], y_s[32 * q : 32 * q + 4, :].bitcast(I32))
